import numpy as np
import ml_dtypes


def mxq(x, axis, fmt="e4m3"):
    dtype, down = {"e4m3": (ml_dtypes.float8_e4m3fn, 7), "e5m2": (ml_dtypes.float8_e5m2, 14)}[fmt]
    v = np.moveaxis(np.asarray(x, np.float32).astype(ml_dtypes.bfloat16).astype(np.float64), axis, -1)
    blocks = v.reshape(v.shape[:-1] + (-1, 32))
    amax = np.abs(blocks).max(-1, keepdims=True)
    byte = np.maximum(np.where(amax > 0, np.frexp(amax)[1] - 1 + 127, 0) - down, 1)
    scale = np.exp2(byte - 127.0)
    codes = (blocks / scale).astype(np.float32).astype(dtype).astype(np.float64)
    return np.moveaxis((codes * scale).reshape(v.shape), -1, axis)


WIDE = False


def mx_kscale(k):
    if not WIDE:
        return np.ones(k)
    levels = np.array([10, -10, 5, -5, 0])
    if k % 512:
        return np.exp2(np.random.permutation(np.resize(levels, k // 32))).repeat(32)
    a = np.empty((k // 512, 16))
    for p in range(k // 512):
        a[p, :8] = np.random.permutation(np.resize(levels, 8))
        for g in range(8):
            far = levels[np.abs(levels - a[p, g]) >= 10]
            a[p, g + 8] = far[np.random.randint(len(far))]
    return np.exp2(a.ravel()).repeat(32)


def f64(x):
    return np.asarray(x).astype(np.float64)


E2M1 = np.array([0.0, 0.5, 1.0, 1.5, 2.0, 3.0, 4.0, 6.0, -0.0, -0.5, -1.0, -1.5, -2.0, -3.0, -4.0, -6.0])


def pack_weight(w, fmt):
    k, n = w.shape
    w = f64(np.asarray(w, np.float32).astype(ml_dtypes.bfloat16)).reshape(k // 32, 32, n)
    amax = np.abs(w).max(1)
    if fmt == "e4m3":
        byte = np.frexp(amax)[1] - 1 + 127 - 7
    else:
        mant, ex = np.frexp(amax / 6.0)
        byte = np.where(mant > 0.5, ex, ex - 1) + 127
    byte = np.clip(np.where(amax > 0, byte, 1), 1, 254)
    scaled = (w * np.exp2(127.0 - byte)[:, None, :]).reshape(k, n).astype(np.float32)
    by_word = np.ascontiguousarray(scaled.reshape(k // 512, 128, 4, n).transpose(0, 1, 3, 2))
    if fmt == "e4m3":
        words = by_word.astype(ml_dtypes.float8_e4m3fn).view(np.uint8)
    else:
        c = by_word.astype(ml_dtypes.float4_e2m1fn).view(np.uint8) & 0xF
        words = (c[..., 0::2] | (c[..., 1::2] << 4)).reshape(k // 512, 128, 2 * n)
    return np.ascontiguousarray(words), np.ascontiguousarray(byte.astype(np.uint8).reshape(k // 512, 16, n))


def unpack_weight(words, scales, fmt):
    g, _, n = scales.shape
    words = np.ascontiguousarray(words).reshape(g, 128, n, -1)
    if fmt == "e4m3":
        vals = words.view(ml_dtypes.float8_e4m3fn).astype(np.float64)
    else:
        nib = np.empty((g, 128, n, 4), np.uint8)
        nib[..., 0::2] = words & 0xF
        nib[..., 1::2] = words >> 4
        vals = E2M1[nib]
    vals = vals * np.repeat(np.exp2(scales.astype(np.float64) - 127.0), 8, axis=1)[..., None]
    return vals.transpose(0, 1, 3, 2).reshape(g * 512, n)


K, T, J, N = 1024, 512, 512, 512


def setup_inputs():
    n = np.random.standard_normal
    fk = mx_kscale(K)
    fj = mx_kscale(J)
    xtp = pack_weight(n((K, T)) * 0.4 / fk[:, None], "e4m3")
    wsp = pack_weight(n((K, J)) * 1 / np.sqrt(K) * fk[:, None], "e2m1")
    wop = pack_weight(n((J, N)) * 1 / np.sqrt(J) / fj[:, None], "e4m3")
    wyp = pack_weight(n((K, N)) * 2.0 / np.sqrt(K) * fk[:, None], "e2m1")
    return {
        "xt_words": xtp[0],
        "xt_scales": xtp[1],
        "ws_words": wsp[0],
        "ws_scales": wsp[1],
        "fj": (np.random.uniform(64.0, 128.0, (J, 1)) * fj[:, None]).astype(np.float32),
        "wo_words": wop[0],
        "wo_scales": wop[1],
        "wy_words": wyp[0],
        "wy_scales": wyp[1],
    }


def reference(xt_words, xt_scales, ws_words, ws_scales, fj, wo_words, wo_scales, wy_words, wy_scales):
    xtu = unpack_weight(xt_words, xt_scales, "e4m3")
    wsu = unpack_weight(ws_words, ws_scales, "e2m1")
    wou = unpack_weight(wo_words, wo_scales, "e4m3")
    wyu = unpack_weight(wy_words, wy_scales, "e2m1")
    a = xtu.T @ wsu
    e = np.exp(a)
    q = e / np.sum(e, axis=1, keepdims=True)
    qt = q.T
    qw = qt * f64(fj)
    qwq = mxq(qw, 0, "e4m3")
    y = wou.T @ qwq + wyu.T @ xtu
    return y

@@ -1,0 +1,219 @@
+from contextlib import ExitStack
+
+import concourse.mybir as mybir
+from concourse.masks import make_identity
+
+K, T, J, N = 1024, 512, 512, 512
+FLOPS = 2 * K * T * J + 2 * J * N * T + 2 * K * N * T
+
+F32 = mybir.dt.float32
+BF16 = mybir.dt.bfloat16
+I32 = mybir.dt.int32
+U32 = mybir.dt.uint32
+U8 = mybir.dt.uint8
+FP8X4 = mybir.dt.float8_e4m3fn_x4
+FP4X4 = mybir.dt.float4_e2m1fn_x4
+ACT = mybir.ActivationFunctionType
+ALU = mybir.AluOpType
+AX = mybir.AxisListType
+
+P = 128
+Z = K // 512
+TT = T // P
+NT = N // P
+
+
+def tile_mix_shares_carry_slot_rows_kernel(
+    tc, xt_words, xt_scales, ws_words, ws_scales, fj, wo_words, wo_scales, wy_words, wy_scales, out
+):
+    nc = tc.nc
+    with ExitStack() as ctx:
+        sb = ctx.enter_context(tc.tile_pool(name="sb", bufs=1))
+        ps = ctx.enter_context(tc.psum_pool(name="ps", bufs=1))
+        ctx.enter_context(tc.manual_schedule())
+
+        x_codes = sb.tile([P, Z, T], U32, align_bytes=64)
+        s_codes = sb.tile([P, Z, 2 * J], U8, align_bytes=64)
+        y_codes = sb.tile([P, Z, 2 * N], U8, align_bytes=64)
+        o_codes = sb.tile([P, N], U32, align_bytes=64)
+        x_plane = sb.tile([P, Z, T], U8, align_bytes=64)
+        s_plane = sb.tile([P, Z, J], U8, align_bytes=64)
+        y_plane = sb.tile([P, Z, N], U8, align_bytes=64)
+        o_plane = sb.tile([P, 1, N], U8, align_bytes=64)
+        f_cols = sb.tile([P, 4], F32)
+        ident = sb.tile([P, P], F32)
+        warm_in = sb.tile([P, 1], F32)
+        warm_out = sb.tile([P, 1], F32)
+
+        def load_scales(eng, plane, scales, q):
+            eng.dma_start(
+                out=plane[32 * q : 32 * q + 4].bitcast(I32),
+                in_=scales[:, 4 * q : 4 * q + 4, :].rearrange("z r c -> r z c").bitcast(I32),
+            )
+
+        nc.sync.dma_start(out=x_codes[:].bitcast(I32), in_=xt_words.rearrange("z p c r -> p z (c r)").bitcast(I32))
+        nc.gpsimd.dma_start(out=s_codes[:].bitcast(I32), in_=ws_words.rearrange("z p c -> p z c").bitcast(I32))
+        nc.vector.memset(x_plane[:].bitcast(U32), 0)
+        nc.vector.memset(s_plane[:].bitcast(U32), 0)
+        for q in range(4):
+            load_scales(nc.sync if q < 3 else nc.gpsimd, x_plane, xt_scales, q)
+            load_scales(nc.scalar, s_plane, ws_scales, q)
+        nc.vector.memset(warm_in[:], 0.0)
+        nc.scalar.activation(out=warm_out[:], in_=warm_in[:], func=ACT.Exp)
+        nc.vector.memset(ident[:], 0.0)
+        nc.vector.memset(y_plane[:].bitcast(U32), 0)
+        nc.vector.memset(o_plane[:].bitcast(U32), 0)
+        make_identity(nc, ident[:], nomemset=True)
+        nc.sync.dma_start(out=f_cols[:], in_=fj.rearrange("(p r) o -> p (r o)", r=4))
+        nc.sync.dma_start(out=y_codes[:].bitcast(I32), in_=wy_words.rearrange("z p c -> p z c").bitcast(I32))
+        for q in range(4):
+            load_scales(nc.sync, y_plane, wy_scales, q)
+        nc.sync.dma_start(out=o_codes[:].bitcast(I32), in_=wo_words[0].rearrange("p c r -> p (c r)").bitcast(I32))
+        for q in range(4):
+            load_scales(nc.sync, o_plane, wo_scales, q)
+
+        def cols(i):
+            return slice(i * P, (i + 1) * P)
+
+        scores, neg_max, expo, total, inv, qw, turned, grouped, q_codes, q_plane, acc = (dict() for d in range(11))
+
+        def score(i):
+            scores[i] = ps.tile([P, J], F32, name="scores%d" % i, tag="bank%d" % i)
+            for z in range(Z):
+                nc.tensor.matmul_mx(
+                    out=scores[i][:],
+                    lhsT=x_codes[:, z, cols(i)].bitcast(FP8X4),
+                    lhsT_scale=x_plane[:, z, cols(i)],
+                    rhs=s_codes[:, z, :].bitcast(FP4X4),
+                    rhs_scale=s_plane[:, z, :],
+                    start=(z == 0),
+                    stop=(z == Z - 1),
+                )
+
+        def row_max(i):
+            neg_max[i] = sb.tile([P, 1], F32, name="neg_max%d" % i)
+            nc.vector.tensor_reduce(out=neg_max[i][:], in_=scores[i][:], axis=AX.X, op=ALU.max, negate=True)
+
+        def exponent(i):
+            expo[i] = sb.tile([P, J], F32, name="expo%d" % i)
+            total[i] = sb.tile([P, 1], F32, name="total%d" % i)
+            nc.scalar.activation(
+                out=expo[i][:].rearrange("t (u p e) -> t u p e", u=2, e=2),
+                in_=scores[i][:].rearrange("t (p u e) -> t u p e", u=2, e=2),
+                func=ACT.Exp,
+                bias=neg_max[i][:],
+                accum_out=total[i][:],
+            )
+
+        def invert(i):
+            inv[i] = sb.tile([P, 1], F32, name="inv%d" % i)
+            nc.vector.reciprocal(out=inv[i][:], in_=total[i][:])
+
+        def weigh(i):
+            qw[i] = sb.tile([P, J], BF16, name="qw%d" % i)
+            nc.vector.scalar_tensor_tensor(
+                out=qw[i][:], in0=expo[i][:], scalar=inv[i][:], in1=f_rows[:], op0=ALU.mult, op1=ALU.mult
+            )
+
+        def turn(i):
+            turned[i] = ps.tile([P, 2, P], F32, name="turned%d" % i, tag="bank%d" % i)
+            words = qw[i][:].bitcast(F32)
+            for u in range(2):
+                nc.tensor.transpose(turned[i][:, u, :], words[:, cols(u)], ident[:])
+
+        def gather(i):
+            grouped[i] = sb.tile([P, 4 * P], BF16, name="grouped%d" % i, align_bytes=64)
+            nc.scalar.copy(
+                out=grouped[i][:].bitcast(F32).rearrange("p (t u) -> p t u", u=2),
+                in_=turned[i][:].rearrange("p u t -> p t u"),
+            )
+
+        def quantize(i):
+            q_codes[i] = sb.tile([P, P], U32, name="q_codes%d" % i, align_bytes=64)
+            q_plane[i] = sb.tile([P, P], U8, name="q_plane%d" % i, align_bytes=64)
+            nc.vector.quantize_mx(out=q_codes[i][:].bitcast(FP8X4), scales=q_plane[i][:], in_=grouped[i][:])
+
+        def own_product(i):
+            acc[i] = ps.tile([P, NT, P], F32, name="acc%d" % i, tag="bank%d" % ((4 + i) if i < 3 else 0))
+            for m in range(NT):
+                for z in range(Z):
+                    nc.tensor.matmul_mx(
+                        out=acc[i][:, m, :],
+                        lhsT=y_codes[:, z, 2 * P * m : 2 * P * (m + 1)].bitcast(FP4X4),
+                        lhsT_scale=y_plane[:, z, cols(m)],
+                        rhs=x_codes[:, z, cols(i)].bitcast(FP8X4),
+                        rhs_scale=x_plane[:, z, cols(i)],
+                        start=(m == 0 and z == 0),
+                        stop=False,
+                    )
+
+        def mix(i):
+            for m in range(NT):
+                nc.tensor.matmul_mx(
+                    out=acc[i][:, m, :],
+                    lhsT=o_codes[:, cols(m)].bitcast(FP8X4),
+                    lhsT_scale=o_plane[:, 0, cols(m)],
+                    rhs=q_codes[i][:].bitcast(FP8X4),
+                    rhs_scale=q_plane[i][:],
+                    start=False,
+                    stop=(m == NT - 1),
+                )
+
+        out_v = out.rearrange("(m p) t -> p m t", p=P)
+
+        def store(i, on_vector):
+            result = sb.tile([P, NT, P], F32, name="result%d" % i)
+            if on_vector:
+                nc.vector.tensor_copy(out=result[:], in_=acc[i][:])
+            else:
+                nc.scalar.copy(out=result[:], in_=acc[i][:])
+            nc.sync.dma_start(out=out_v[:, :, cols(i)], in_=result[:])
+
+        score(0)
+        row_max(0)
+        exponent(0)
+        score(1)
+        row_max(1)
+        exponent(1)
+        score(2)
+        invert(0)
+        row_max(2)
+        exponent(2)
+        score(3)
+        f_rows = ps.tile([P, J], F32, tag="bank7")
+        f_view = f_rows[:].rearrange("m (u p e) -> m u e p", u=2, e=2)
+        for r in range(4):
+            nc.tensor.transpose(f_view[:, r // 2, r % 2, :], f_cols[:, r : r + 1].to_broadcast([P, P]), ident[:])
+        weigh(0)
+        invert(1)
+        row_max(3)
+        own_product(0)
+        turn(0)
+        gather(0)
+        exponent(3)
+        weigh(1)
+        own_product(1)
+        turn(1)
+        invert(2)
+        quantize(0)
+        gather(1)
+        mix(0)
+        weigh(2)
+        own_product(2)
+        turn(2)
+        invert(3)
+        quantize(1)
+        store(0, False)
+        gather(2)
+        mix(1)
+        weigh(3)
+        own_product(3)
+        turn(3)
+        quantize(2)
+        mix(2)
+        gather(3)
+        store(1, True)
+        quantize(3)
+        store(2, False)
+        mix(3)
+        store(3, True)

@@ -21,6 +21,8 @@ P = 128
 Z = K // 512
 TT = T // P
 NT = N // P
+WARM_A = 8
+WARM_B = 8
 
 
 def tile_mix_shares_carry_slot_rows_kernel(
@@ -51,26 +53,59 @@ def tile_mix_shares_carry_slot_rows_kernel(
                 in_=scales[:, 4 * q : 4 * q + 4, :].rearrange("z r c -> r z c").bitcast(I32),
             )
 
-        nc.sync.dma_start(out=x_codes[:].bitcast(I32), in_=xt_words.rearrange("z p c r -> p z (c r)").bitcast(I32))
-        nc.gpsimd.dma_start(out=s_codes[:].bitcast(I32), in_=ws_words.rearrange("z p c -> p z c").bitcast(I32))
+        nc.sync.dma_start(out=f_cols[:], in_=fj.rearrange("(p r) o -> p (r o)", r=4))
         nc.vector.memset(x_plane[:].bitcast(U32), 0)
-        nc.vector.memset(s_plane[:].bitcast(U32), 0)
-        for q in range(4):
-            load_scales(nc.sync if q < 3 else nc.gpsimd, x_plane, xt_scales, q)
+        nc.gpsimd.memset(s_plane[:].bitcast(U32), 0)
+        nc.gpsimd.memset(y_plane[:].bitcast(U32), 0)
+        nc.gpsimd.memset(o_plane[:].bitcast(U32), 0)
+        for q in range(2):
+            load_scales(nc.sync, x_plane, xt_scales, q)
+        for q in range(3):
             load_scales(nc.scalar, s_plane, ws_scales, q)
+        nc.sync.dma_start(out=x_codes[:].bitcast(I32), in_=xt_words.rearrange("z p c r -> p z (c r)").bitcast(I32))
+        nc.sync.dma_start(out=s_codes[:].bitcast(I32), in_=ws_words.rearrange("z p c -> p z c").bitcast(I32))
+        for q in range(2, 4):
+            load_scales(nc.sync, x_plane, xt_scales, q)
+        load_scales(nc.sync, s_plane, ws_scales, 3)
         nc.vector.memset(warm_in[:], 0.0)
         nc.scalar.activation(out=warm_out[:], in_=warm_in[:], func=ACT.Exp)
-        nc.vector.memset(ident[:], 0.0)
-        nc.vector.memset(y_plane[:].bitcast(U32), 0)
-        nc.vector.memset(o_plane[:].bitcast(U32), 0)
-        make_identity(nc, ident[:], nomemset=True)
-        nc.sync.dma_start(out=f_cols[:], in_=fj.rearrange("(p r) o -> p (r o)", r=4))
-        nc.sync.dma_start(out=y_codes[:].bitcast(I32), in_=wy_words.rearrange("z p c -> p z c").bitcast(I32))
+        ones = sb.tile([P, 4 * P], BF16, align_bytes=64)
+        one_codes = sb.tile([P, P], U32, align_bytes=64)
+        one_plane = sb.tile([P, P], U8, align_bytes=64)
+        nc.vector.memset(ones[:], 1.0)
+        nc.vector.quantize_mx(out=one_codes[:].bitcast(FP8X4), scales=one_plane[:], in_=ones[:])
+        make_identity(nc, ident[:])
         for q in range(4):
             load_scales(nc.sync, y_plane, wy_scales, q)
+        nc.sync.dma_start(out=y_codes[:].bitcast(I32), in_=wy_words.rearrange("z p c -> p z c").bitcast(I32))
         nc.sync.dma_start(out=o_codes[:].bitcast(I32), in_=wo_words[0].rearrange("p c r -> p (c r)").bitcast(I32))
         for q in range(4):
             load_scales(nc.sync, o_plane, wo_scales, q)
+
+        idle = ps.tile([P, P], F32, tag="bank6")
+
+        def warm(n):
+            for w in range(n):
+                nc.tensor.matmul_mx(
+                    out=idle[:],
+                    lhsT=one_codes[:].bitcast(FP8X4),
+                    lhsT_scale=one_plane[:],
+                    rhs=one_codes[:].bitcast(FP8X4),
+                    rhs_scale=one_plane[:],
+                    start=True,
+                    stop=True,
+                )
+
+        warm(WARM_A)
+        f_spread = ps.tile([P, 4, P], F32, tag="bank7")
+        for r in range(4):
+            nc.tensor.transpose(f_spread[:, r, :], f_cols[:, r : r + 1].to_broadcast([P, P]), ident[:])
+        f_rows = sb.tile([P, J], F32)
+        nc.scalar.copy(
+            out=f_rows[:].rearrange("t (u p e) -> t u p e", u=2, e=2),
+            in_=f_spread[:].rearrange("t (u e) p -> t u p e", u=2),
+        )
+        warm(WARM_B)
 
         def cols(i):
             return slice(i * P, (i + 1) * P)
@@ -134,40 +169,47 @@ def tile_mix_shares_carry_slot_rows_kernel(
             nc.vector.quantize_mx(out=q_codes[i][:].bitcast(FP8X4), scales=q_plane[i][:], in_=grouped[i][:])
 
         def own_product(i):
-            acc[i] = ps.tile([P, NT, P], F32, name="acc%d" % i, tag="bank%d" % ((4 + i) if i < 3 else 0))
+            banks = [4 + i] if i < TT - 1 else [4 + i, 0]
+            per = NT // len(banks)
+            acc[i] = [ps.tile([P, per, P], F32, name="acc%d_%d" % (i, b), tag="bank%d" % b) for b in banks]
             for m in range(NT):
                 for z in range(Z):
                     nc.tensor.matmul_mx(
-                        out=acc[i][:, m, :],
+                        out=acc[i][m // per][:, m % per, :],
                         lhsT=y_codes[:, z, 2 * P * m : 2 * P * (m + 1)].bitcast(FP4X4),
                         lhsT_scale=y_plane[:, z, cols(m)],
                         rhs=x_codes[:, z, cols(i)].bitcast(FP8X4),
                         rhs_scale=x_plane[:, z, cols(i)],
-                        start=(m == 0 and z == 0),
+                        start=(m % per == 0 and z == 0),
                         stop=False,
                     )
 
         def mix(i):
+            per = NT // len(acc[i])
             for m in range(NT):
                 nc.tensor.matmul_mx(
-                    out=acc[i][:, m, :],
+                    out=acc[i][m // per][:, m % per, :],
                     lhsT=o_codes[:, cols(m)].bitcast(FP8X4),
                     lhsT_scale=o_plane[:, 0, cols(m)],
                     rhs=q_codes[i][:].bitcast(FP8X4),
                     rhs_scale=q_plane[i][:],
                     start=False,
-                    stop=(m == NT - 1),
+                    stop=(m % per == per - 1),
                 )
 
         out_v = out.rearrange("(m p) t -> p m t", p=P)
 
         def store(i, on_vector):
-            result = sb.tile([P, NT, P], F32, name="result%d" % i)
-            if on_vector:
-                nc.vector.tensor_copy(out=result[:], in_=acc[i][:])
-            else:
-                nc.scalar.copy(out=result[:], in_=acc[i][:])
-            nc.sync.dma_start(out=out_v[:, :, cols(i)], in_=result[:])
+            per = NT // len(acc[i])
+            for b, bank in enumerate(acc[i]):
+                result = sb.tile([P, per, P], F32, name="result%d_%d" % (i, b))
+                rows = out_v[:, b * per : (b + 1) * per, cols(i)]
+                if on_vector == (b == 0):
+                    nc.vector.tensor_copy(out=result[:], in_=bank[:])
+                    nc.sync.dma_start(out=rows, in_=result[:])
+                else:
+                    nc.scalar.copy(out=result[:], in_=bank[:])
+                    nc.scalar.dma_start(out=rows, in_=result[:])
 
         score(0)
         row_max(0)
@@ -176,44 +218,40 @@ def tile_mix_shares_carry_slot_rows_kernel(
         row_max(1)
         exponent(1)
         score(2)
-        invert(0)
         row_max(2)
         exponent(2)
+        invert(0)
         score(3)
-        f_rows = ps.tile([P, J], F32, tag="bank7")
-        f_view = f_rows[:].rearrange("m (u p e) -> m u e p", u=2, e=2)
-        for r in range(4):
-            nc.tensor.transpose(f_view[:, r // 2, r % 2, :], f_cols[:, r : r + 1].to_broadcast([P, P]), ident[:])
-        weigh(0)
-        invert(1)
         row_max(3)
+        exponent(3)
         own_product(0)
+        own_product(1)
+        invert(1)
+        weigh(0)
         turn(0)
         gather(0)
-        exponent(3)
-        weigh(1)
-        own_product(1)
-        turn(1)
         invert(2)
-        quantize(0)
-        gather(1)
-        mix(0)
-        weigh(2)
+        weigh(1)
         own_product(2)
-        turn(2)
+        turn(1)
         invert(3)
-        quantize(1)
-        store(0, False)
-        gather(2)
-        mix(1)
+        weigh(2)
+        turn(2)
+        gather(1)
+        quantize(0)
+        mix(0)
         weigh(3)
-        own_product(3)
+        gather(2)
         turn(3)
+        quantize(1)
+        mix(1)
         quantize(2)
         mix(2)
+        own_product(3)
         gather(3)
-        store(1, True)
+        store(0, True)
+        store(1, False)
         quantize(3)
-        store(2, False)
         mix(3)
-        store(3, True)
+        store(2, True)
+        store(3, False)

@@ -44,7 +44,6 @@ def tile_mix_shares_carry_slot_rows_kernel(
         o_plane = sb.tile([P, 1, N], U8, align_bytes=64)
         f_cols = sb.tile([P, 4], F32)
         ident = sb.tile([P, P], F32)
-        warm_in = sb.tile([P, 1], F32)
         warm_out = sb.tile([P, 1], F32)
 
         def load_scales(eng, plane, scales, q):
@@ -67,17 +66,16 @@ def tile_mix_shares_carry_slot_rows_kernel(
         for q in range(2, 4):
             load_scales(nc.sync, x_plane, xt_scales, q)
         load_scales(nc.sync, s_plane, ws_scales, 3)
-        nc.vector.memset(warm_in[:], 0.0)
-        nc.scalar.activation(out=warm_out[:], in_=warm_in[:], func=ACT.Exp)
         ones = sb.tile([P, 4 * P], BF16, align_bytes=64)
         one_codes = sb.tile([P, P], U32, align_bytes=64)
         one_plane = sb.tile([P, P], U8, align_bytes=64)
         nc.vector.memset(ones[:], 1.0)
+        nc.scalar.activation(out=warm_out[:], in_=ones[:, 0:1], func=ACT.Exp)
         nc.vector.quantize_mx(out=one_codes[:].bitcast(FP8X4), scales=one_plane[:], in_=ones[:])
         make_identity(nc, ident[:])
+        nc.sync.dma_start(out=y_codes[:].bitcast(I32), in_=wy_words.rearrange("z p c -> p z c").bitcast(I32))
         for q in range(4):
             load_scales(nc.sync, y_plane, wy_scales, q)
-        nc.sync.dma_start(out=y_codes[:].bitcast(I32), in_=wy_words.rearrange("z p c -> p z c").bitcast(I32))
         nc.sync.dma_start(out=o_codes[:].bitcast(I32), in_=wo_words[0].rearrange("p c r -> p (c r)").bitcast(I32))
         for q in range(4):
             load_scales(nc.sync, o_plane, wo_scales, q)
@@ -199,17 +197,16 @@ def tile_mix_shares_carry_slot_rows_kernel(
 
         out_v = out.rearrange("(m p) t -> p m t", p=P)
 
-        def store(i, on_vector):
+        def store(i, h, on_vector):
             per = NT // len(acc[i])
-            for b, bank in enumerate(acc[i]):
-                result = sb.tile([P, per, P], F32, name="result%d_%d" % (i, b))
-                rows = out_v[:, b * per : (b + 1) * per, cols(i)]
-                if on_vector == (b == 0):
-                    nc.vector.tensor_copy(out=result[:], in_=bank[:])
-                    nc.sync.dma_start(out=rows, in_=result[:])
-                else:
-                    nc.scalar.copy(out=result[:], in_=bank[:])
-                    nc.scalar.dma_start(out=rows, in_=result[:])
+            result = sb.tile([P, 2, P], F32, name="result%d_%d" % (i, h))
+            rows = out_v[:, 2 * h : 2 * h + 2, cols(i)]
+            src = acc[i][2 * h // per][:, (2 * h) % per : (2 * h) % per + 2, :]
+            if on_vector:
+                nc.vector.tensor_copy(out=result[:], in_=src)
+            else:
+                nc.scalar.copy(out=result[:], in_=src)
+            (nc.scalar if i == TT - 1 and not on_vector else nc.sync).dma_start(out=rows, in_=result[:])
 
         score(0)
         row_max(0)
@@ -248,10 +245,14 @@ def tile_mix_shares_carry_slot_rows_kernel(
         quantize(2)
         mix(2)
         own_product(3)
+        store(0, 0, False)
+        store(0, 1, False)
         gather(3)
-        store(0, True)
-        store(1, False)
+        store(1, 0, True)
         quantize(3)
+        store(1, 1, True)
         mix(3)
-        store(2, True)
-        store(3, False)
+        store(2, 0, False)
+        store(2, 1, False)
+        store(3, 0, False)
+        store(3, 1, True)

@@ -21,8 +21,8 @@ P = 128
 Z = K // 512
 TT = T // P
 NT = N // P
-WARM_A = 8
-WARM_B = 8
+WARM_A = 10
+WARM_B = 7
 
 
 def tile_mix_shares_carry_slot_rows_kernel(
@@ -34,7 +34,7 @@ def tile_mix_shares_carry_slot_rows_kernel(
         ps = ctx.enter_context(tc.psum_pool(name="ps", bufs=1))
         ctx.enter_context(tc.manual_schedule())
 
-        x_codes = sb.tile([P, Z, T], U32, align_bytes=64)
+        x_halves = [sb.tile([P, Z, T // 2], U32, name="x_codes%d" % h, align_bytes=64) for h in range(2)]
         s_codes = sb.tile([P, Z, 2 * J], U8, align_bytes=64)
         y_codes = sb.tile([P, Z, 2 * N], U8, align_bytes=64)
         o_codes = sb.tile([P, N], U32, align_bytes=64)
@@ -48,31 +48,40 @@ def tile_mix_shares_carry_slot_rows_kernel(
 
         def load_scales(eng, plane, scales, q):
             eng.dma_start(
-                out=plane[32 * q : 32 * q + 4].bitcast(I32),
-                in_=scales[:, 4 * q : 4 * q + 4, :].rearrange("z r c -> r z c").bitcast(I32),
+                out=plane[q:P:32].bitcast(I32),
+                in_=scales[:, q:16:4, :].rearrange("z r c -> r z c").bitcast(I32),
             )
+
+        def load_tokens(h):
+            words = xt_words[:, :, h * (T // 2) : (h + 1) * (T // 2), :].rearrange("z p c r -> p z (c r)")
+            nc.sync.dma_start(out=x_halves[h][:].bitcast(I32), in_=words.bitcast(I32))
+
+        def x_codes(z, i):
+            return x_halves[i // 2][:, z, (i % 2) * P : (i % 2 + 1) * P].bitcast(FP8X4)
 
         nc.sync.dma_start(out=f_cols[:], in_=fj.rearrange("(p r) o -> p (r o)", r=4))
         nc.vector.memset(x_plane[:].bitcast(U32), 0)
-        nc.gpsimd.memset(s_plane[:].bitcast(U32), 0)
-        nc.gpsimd.memset(y_plane[:].bitcast(U32), 0)
-        nc.gpsimd.memset(o_plane[:].bitcast(U32), 0)
+        nc.vector.memset(s_plane[:].bitcast(U32), 0)
         for q in range(2):
             load_scales(nc.sync, x_plane, xt_scales, q)
-        for q in range(3):
-            load_scales(nc.scalar, s_plane, ws_scales, q)
-        nc.sync.dma_start(out=x_codes[:].bitcast(I32), in_=xt_words.rearrange("z p c r -> p z (c r)").bitcast(I32))
+        load_tokens(0)
         nc.sync.dma_start(out=s_codes[:].bitcast(I32), in_=ws_words.rearrange("z p c -> p z c").bitcast(I32))
+        for q in range(3):
+            load_scales(nc.sync, s_plane, ws_scales, q)
         for q in range(2, 4):
             load_scales(nc.sync, x_plane, xt_scales, q)
         load_scales(nc.sync, s_plane, ws_scales, 3)
         ones = sb.tile([P, 4 * P], BF16, align_bytes=64)
         one_codes = sb.tile([P, P], U32, align_bytes=64)
         one_plane = sb.tile([P, P], U8, align_bytes=64)
-        nc.vector.memset(ones[:], 1.0)
+        nc.gpsimd.memset(ones[:].bitcast(U32), 0x3F803F80)
         nc.scalar.activation(out=warm_out[:], in_=ones[:, 0:1], func=ACT.Exp)
         nc.vector.quantize_mx(out=one_codes[:].bitcast(FP8X4), scales=one_plane[:], in_=ones[:])
-        make_identity(nc, ident[:])
+        nc.vector.memset(ident[:], 0.0)
+        make_identity(nc, ident[:], nomemset=True)
+        nc.vector.memset(y_plane[:].bitcast(U32), 0)
+        nc.vector.memset(o_plane[:].bitcast(U32), 0)
+        load_tokens(1)
         nc.sync.dma_start(out=y_codes[:].bitcast(I32), in_=wy_words.rearrange("z p c -> p z c").bitcast(I32))
         for q in range(4):
             load_scales(nc.sync, y_plane, wy_scales, q)
@@ -115,7 +124,7 @@ def tile_mix_shares_carry_slot_rows_kernel(
             for z in range(Z):
                 nc.tensor.matmul_mx(
                     out=scores[i][:],
-                    lhsT=x_codes[:, z, cols(i)].bitcast(FP8X4),
+                    lhsT=x_codes(z, i),
                     lhsT_scale=x_plane[:, z, cols(i)],
                     rhs=s_codes[:, z, :].bitcast(FP4X4),
                     rhs_scale=s_plane[:, z, :],
@@ -176,7 +185,7 @@ def tile_mix_shares_carry_slot_rows_kernel(
                         out=acc[i][m // per][:, m % per, :],
                         lhsT=y_codes[:, z, 2 * P * m : 2 * P * (m + 1)].bitcast(FP4X4),
                         lhsT_scale=y_plane[:, z, cols(m)],
-                        rhs=x_codes[:, z, cols(i)].bitcast(FP8X4),
+                        rhs=x_codes(z, i),
                         rhs_scale=x_plane[:, z, cols(i)],
                         start=(m % per == 0 and z == 0),
                         stop=False,

@@ -18,11 +18,20 @@ ALU = mybir.AluOpType
 AX = mybir.AxisListType
 
 P = 128
-Z = K // 512
-TT = T // P
-NT = N // P
-WARM_A = 10
-WARM_B = 7
+PACK = 4
+PASSES = K // (P * PACK)
+TOKEN_TILES = T // P
+FEATURE_TILES = N // P
+LAST = TOKEN_TILES - 1
+QUADRANT = 32
+SCALE_ROWS = 16
+BF16_ONE_PAIR = 0x3F803F80
+WARM_PASSES_BEFORE_SPREAD = 10
+WARM_PASSES_AFTER_SPREAD = 9
+
+
+def block(i):
+    return slice(i * P, (i + 1) * P)
 
 
 def tile_mix_shares_carry_slot_rows_kernel(
@@ -34,102 +43,99 @@ def tile_mix_shares_carry_slot_rows_kernel(
         ps = ctx.enter_context(tc.psum_pool(name="ps", bufs=1))
         ctx.enter_context(tc.manual_schedule())
 
-        x_halves = [sb.tile([P, Z, T // 2], U32, name="x_codes%d" % h, align_bytes=64) for h in range(2)]
-        s_codes = sb.tile([P, Z, 2 * J], U8, align_bytes=64)
-        y_codes = sb.tile([P, Z, 2 * N], U8, align_bytes=64)
-        o_codes = sb.tile([P, N], U32, align_bytes=64)
-        x_plane = sb.tile([P, Z, T], U8, align_bytes=64)
-        s_plane = sb.tile([P, Z, J], U8, align_bytes=64)
-        y_plane = sb.tile([P, Z, N], U8, align_bytes=64)
-        o_plane = sb.tile([P, 1, N], U8, align_bytes=64)
-        f_cols = sb.tile([P, 4], F32)
+        xt_halves = [sb.tile([P, PASSES, T // 2], U32, name="xt_half%d" % h, align_bytes=64) for h in range(2)]
+        ws_codes = sb.tile([P, PASSES, 2 * J], U8, align_bytes=64)
+        wy_codes = sb.tile([P, PASSES, 2 * N], U8, align_bytes=64)
+        wo_codes = sb.tile([P, N], U32, align_bytes=64)
+        xt_plane = sb.tile([P, PASSES, T], U8, align_bytes=64)
+        ws_plane = sb.tile([P, PASSES, J], U8, align_bytes=64)
+        wy_plane = sb.tile([P, PASSES, N], U8, align_bytes=64)
+        wo_plane = sb.tile([P, 1, N], U8, align_bytes=64)
+        fj_cols = sb.tile([P, PACK], F32)
         ident = sb.tile([P, P], F32)
-        warm_out = sb.tile([P, 1], F32)
 
-        def load_scales(eng, plane, scales, q):
-            eng.dma_start(
-                out=plane[q:P:32].bitcast(I32),
-                in_=scales[:, q:16:4, :].rearrange("z r c -> r z c").bitcast(I32),
+        def load_scales(plane, scales, r):
+            nc.sync.dma_start(
+                out=plane[r:P:QUADRANT].bitcast(I32),
+                in_=scales[:, r:SCALE_ROWS:PACK, :].rearrange("z q c -> q z c").bitcast(I32),
             )
 
         def load_tokens(h):
             words = xt_words[:, :, h * (T // 2) : (h + 1) * (T // 2), :].rearrange("z p c r -> p z (c r)")
-            nc.sync.dma_start(out=x_halves[h][:].bitcast(I32), in_=words.bitcast(I32))
+            nc.sync.dma_start(out=xt_halves[h][:].bitcast(I32), in_=words.bitcast(I32))
 
-        def x_codes(z, i):
-            return x_halves[i // 2][:, z, (i % 2) * P : (i % 2 + 1) * P].bitcast(FP8X4)
+        def xt_codes(z, i):
+            return xt_halves[i // 2][:, z, block(i % 2)].bitcast(FP8X4)
 
-        nc.sync.dma_start(out=f_cols[:], in_=fj.rearrange("(p r) o -> p (r o)", r=4))
-        nc.vector.memset(x_plane[:].bitcast(U32), 0)
-        nc.vector.memset(s_plane[:].bitcast(U32), 0)
-        for q in range(2):
-            load_scales(nc.sync, x_plane, xt_scales, q)
+        nc.sync.dma_start(out=fj_cols[:], in_=fj.rearrange("(p r) o -> p (r o)", r=PACK))
+        nc.vector.memset(xt_plane[:].bitcast(U32), 0)
+        nc.vector.memset(ws_plane[:].bitcast(U32), 0)
+        for r in range(2):
+            load_scales(xt_plane, xt_scales, r)
         load_tokens(0)
-        nc.sync.dma_start(out=s_codes[:].bitcast(I32), in_=ws_words.rearrange("z p c -> p z c").bitcast(I32))
-        for q in range(3):
-            load_scales(nc.sync, s_plane, ws_scales, q)
-        for q in range(2, 4):
-            load_scales(nc.sync, x_plane, xt_scales, q)
-        load_scales(nc.sync, s_plane, ws_scales, 3)
-        ones = sb.tile([P, 4 * P], BF16, align_bytes=64)
-        one_codes = sb.tile([P, P], U32, align_bytes=64)
-        one_plane = sb.tile([P, P], U8, align_bytes=64)
-        nc.gpsimd.memset(ones[:].bitcast(U32), 0x3F803F80)
-        nc.scalar.activation(out=warm_out[:], in_=ones[:, 0:1], func=ACT.Exp)
-        nc.vector.quantize_mx(out=one_codes[:].bitcast(FP8X4), scales=one_plane[:], in_=ones[:])
+        nc.sync.dma_start(out=ws_codes[:].bitcast(I32), in_=ws_words.rearrange("z p c -> p z c").bitcast(I32))
+        for r in range(3):
+            load_scales(ws_plane, ws_scales, r)
+        for r in range(2, PACK):
+            load_scales(xt_plane, xt_scales, r)
+        load_scales(ws_plane, ws_scales, 3)
+
+        ones = sb.tile([P, PACK * P], BF16, align_bytes=64)
+        ones_codes = sb.tile([P, P], U32, align_bytes=64)
+        ones_plane = sb.tile([P, P], U8, align_bytes=64)
+        nc.gpsimd.memset(ones[:].bitcast(U32), BF16_ONE_PAIR)
+        nc.vector.quantize_mx(out=ones_codes[:].bitcast(FP8X4), scales=ones_plane[:], in_=ones[:])
         nc.vector.memset(ident[:], 0.0)
         make_identity(nc, ident[:], nomemset=True)
-        nc.vector.memset(y_plane[:].bitcast(U32), 0)
-        nc.vector.memset(o_plane[:].bitcast(U32), 0)
+        nc.vector.memset(wy_plane[:].bitcast(U32), 0)
+        nc.vector.memset(wo_plane[:].bitcast(U32), 0)
+
         load_tokens(1)
-        nc.sync.dma_start(out=y_codes[:].bitcast(I32), in_=wy_words.rearrange("z p c -> p z c").bitcast(I32))
-        for q in range(4):
-            load_scales(nc.sync, y_plane, wy_scales, q)
-        nc.sync.dma_start(out=o_codes[:].bitcast(I32), in_=wo_words[0].rearrange("p c r -> p (c r)").bitcast(I32))
-        for q in range(4):
-            load_scales(nc.sync, o_plane, wo_scales, q)
+        nc.sync.dma_start(out=wy_codes[:].bitcast(I32), in_=wy_words.rearrange("z p c -> p z c").bitcast(I32))
+        for r in range(PACK):
+            load_scales(wy_plane, wy_scales, r)
+        nc.sync.dma_start(out=wo_codes[:].bitcast(I32), in_=wo_words[0].rearrange("p c r -> p (c r)").bitcast(I32))
+        for r in range(PACK):
+            load_scales(wo_plane, wo_scales, r)
 
-        idle = ps.tile([P, P], F32, tag="bank6")
+        warm_sums = ps.tile([P, P], F32, tag="bank6")
 
-        def warm(n):
-            for w in range(n):
+        def warm_up(passes):
+            for n in range(passes):
                 nc.tensor.matmul_mx(
-                    out=idle[:],
-                    lhsT=one_codes[:].bitcast(FP8X4),
-                    lhsT_scale=one_plane[:],
-                    rhs=one_codes[:].bitcast(FP8X4),
-                    rhs_scale=one_plane[:],
+                    out=warm_sums[:],
+                    lhsT=ones_codes[:].bitcast(FP8X4),
+                    lhsT_scale=ones_plane[:],
+                    rhs=ones_codes[:].bitcast(FP8X4),
+                    rhs_scale=ones_plane[:],
                     start=True,
                     stop=True,
                 )
 
-        warm(WARM_A)
-        f_spread = ps.tile([P, 4, P], F32, tag="bank7")
-        for r in range(4):
-            nc.tensor.transpose(f_spread[:, r, :], f_cols[:, r : r + 1].to_broadcast([P, P]), ident[:])
-        f_rows = sb.tile([P, J], F32)
+        warm_up(WARM_PASSES_BEFORE_SPREAD)
+        fj_spread = ps.tile([P, PACK, P], F32, tag="bank7")
+        for r in range(PACK):
+            nc.tensor.transpose(fj_spread[:, r, :], fj_cols[:, r : r + 1].to_broadcast([P, P]), ident[:])
+        fj_rows = sb.tile([P, J], F32)
         nc.scalar.copy(
-            out=f_rows[:].rearrange("t (u p e) -> t u p e", u=2, e=2),
-            in_=f_spread[:].rearrange("t (u e) p -> t u p e", u=2),
+            out=fj_rows[:].rearrange("t (u p e) -> t u p e", u=2, e=2),
+            in_=fj_spread[:].rearrange("t (u e) p -> t u p e", u=2),
         )
-        warm(WARM_B)
+        warm_up(WARM_PASSES_AFTER_SPREAD)
 
-        def cols(i):
-            return slice(i * P, (i + 1) * P)
-
-        scores, neg_max, expo, total, inv, qw, turned, grouped, q_codes, q_plane, acc = (dict() for d in range(11))
+        scores, neg_max, expo, total, inv, qw, turned, grouped, qw_codes, qw_plane, sums = (dict() for d in range(11))
 
         def score(i):
             scores[i] = ps.tile([P, J], F32, name="scores%d" % i, tag="bank%d" % i)
-            for z in range(Z):
+            for z in range(PASSES):
                 nc.tensor.matmul_mx(
                     out=scores[i][:],
-                    lhsT=x_codes(z, i),
-                    lhsT_scale=x_plane[:, z, cols(i)],
-                    rhs=s_codes[:, z, :].bitcast(FP4X4),
-                    rhs_scale=s_plane[:, z, :],
+                    lhsT=xt_codes(z, i),
+                    lhsT_scale=xt_plane[:, z, block(i)],
+                    rhs=ws_codes[:, z, :].bitcast(FP4X4),
+                    rhs_scale=ws_plane[:, z, :],
                     start=(z == 0),
-                    stop=(z == Z - 1),
+                    stop=(z == PASSES - 1),
                 )
 
         def row_max(i):
@@ -154,82 +160,74 @@ def tile_mix_shares_carry_slot_rows_kernel(
         def weigh(i):
             qw[i] = sb.tile([P, J], BF16, name="qw%d" % i)
             nc.vector.scalar_tensor_tensor(
-                out=qw[i][:], in0=expo[i][:], scalar=inv[i][:], in1=f_rows[:], op0=ALU.mult, op1=ALU.mult
+                out=qw[i][:], in0=expo[i][:], scalar=inv[i][:], in1=fj_rows[:], op0=ALU.mult, op1=ALU.mult
             )
 
         def turn(i):
             turned[i] = ps.tile([P, 2, P], F32, name="turned%d" % i, tag="bank%d" % i)
-            words = qw[i][:].bitcast(F32)
+            pairs = qw[i][:].bitcast(F32)
             for u in range(2):
-                nc.tensor.transpose(turned[i][:, u, :], words[:, cols(u)], ident[:])
+                nc.tensor.transpose(turned[i][:, u, :], pairs[:, block(u)], ident[:])
 
         def gather(i):
-            grouped[i] = sb.tile([P, 4 * P], BF16, name="grouped%d" % i, align_bytes=64)
+            grouped[i] = sb.tile([P, PACK * P], BF16, name="grouped%d" % i, align_bytes=64)
             nc.scalar.copy(
                 out=grouped[i][:].bitcast(F32).rearrange("p (t u) -> p t u", u=2),
                 in_=turned[i][:].rearrange("p u t -> p t u"),
             )
 
         def quantize(i):
-            q_codes[i] = sb.tile([P, P], U32, name="q_codes%d" % i, align_bytes=64)
-            q_plane[i] = sb.tile([P, P], U8, name="q_plane%d" % i, align_bytes=64)
-            nc.vector.quantize_mx(out=q_codes[i][:].bitcast(FP8X4), scales=q_plane[i][:], in_=grouped[i][:])
+            qw_codes[i] = sb.tile([P, P], U32, name="qw_codes%d" % i, align_bytes=64)
+            qw_plane[i] = sb.tile([P, P], U8, name="qw_plane%d" % i, align_bytes=64)
+            nc.vector.quantize_mx(out=qw_codes[i][:].bitcast(FP8X4), scales=qw_plane[i][:], in_=grouped[i][:])
 
         def own_product(i):
-            banks = [4 + i] if i < TT - 1 else [4 + i, 0]
-            per = NT // len(banks)
-            acc[i] = [ps.tile([P, per, P], F32, name="acc%d_%d" % (i, b), tag="bank%d" % b) for b in banks]
-            for m in range(NT):
-                for z in range(Z):
+            banks = [TOKEN_TILES + i] if i < LAST else [TOKEN_TILES + i, 0]
+            per_bank = FEATURE_TILES // len(banks)
+            sums[i] = [ps.tile([P, per_bank, P], F32, name="sums%d_%d" % (i, b), tag="bank%d" % b) for b in banks]
+            for m in range(FEATURE_TILES):
+                for z in range(PASSES):
                     nc.tensor.matmul_mx(
-                        out=acc[i][m // per][:, m % per, :],
-                        lhsT=y_codes[:, z, 2 * P * m : 2 * P * (m + 1)].bitcast(FP4X4),
-                        lhsT_scale=y_plane[:, z, cols(m)],
-                        rhs=x_codes(z, i),
-                        rhs_scale=x_plane[:, z, cols(i)],
-                        start=(m % per == 0 and z == 0),
+                        out=sums[i][m // per_bank][:, m % per_bank, :],
+                        lhsT=wy_codes[:, z, 2 * P * m : 2 * P * (m + 1)].bitcast(FP4X4),
+                        lhsT_scale=wy_plane[:, z, block(m)],
+                        rhs=xt_codes(z, i),
+                        rhs_scale=xt_plane[:, z, block(i)],
+                        start=(m % per_bank == 0 and z == 0),
                         stop=False,
                     )
 
         def mix(i):
-            per = NT // len(acc[i])
-            for m in range(NT):
+            per_bank = FEATURE_TILES // len(sums[i])
+            for m in range(FEATURE_TILES):
                 nc.tensor.matmul_mx(
-                    out=acc[i][m // per][:, m % per, :],
-                    lhsT=o_codes[:, cols(m)].bitcast(FP8X4),
-                    lhsT_scale=o_plane[:, 0, cols(m)],
-                    rhs=q_codes[i][:].bitcast(FP8X4),
-                    rhs_scale=q_plane[i][:],
+                    out=sums[i][m // per_bank][:, m % per_bank, :],
+                    lhsT=wo_codes[:, block(m)].bitcast(FP8X4),
+                    lhsT_scale=wo_plane[:, 0, block(m)],
+                    rhs=qw_codes[i][:].bitcast(FP8X4),
+                    rhs_scale=qw_plane[i][:],
                     start=False,
-                    stop=(m % per == per - 1),
+                    stop=(m % per_bank == per_bank - 1),
                 )
 
-        out_v = out.rearrange("(m p) t -> p m t", p=P)
+        out_tiles = out.rearrange("(m p) t -> p m t", p=P)
 
-        def store(i, h, on_vector):
-            per = NT // len(acc[i])
+        def store(i, h, copy, queue):
+            per_bank = FEATURE_TILES // len(sums[i])
             result = sb.tile([P, 2, P], F32, name="result%d_%d" % (i, h))
-            rows = out_v[:, 2 * h : 2 * h + 2, cols(i)]
-            src = acc[i][2 * h // per][:, (2 * h) % per : (2 * h) % per + 2, :]
-            if on_vector:
-                nc.vector.tensor_copy(out=result[:], in_=src)
-            else:
-                nc.scalar.copy(out=result[:], in_=src)
-            (nc.scalar if i == TT - 1 and not on_vector else nc.sync).dma_start(out=rows, in_=result[:])
+            bank, first = divmod(2 * h, per_bank)
+            copy(out=result[:], in_=sums[i][bank][:, first : first + 2, :])
+            queue.dma_start(out=out_tiles[:, 2 * h : 2 * h + 2, block(i)], in_=result[:])
 
-        score(0)
-        row_max(0)
-        exponent(0)
-        score(1)
-        row_max(1)
-        exponent(1)
-        score(2)
-        row_max(2)
-        exponent(2)
-        invert(0)
-        score(3)
-        row_max(3)
-        exponent(3)
+        on_scalar, on_vector = nc.scalar.copy, nc.vector.tensor_copy
+
+        for i in range(TOKEN_TILES):
+            score(i)
+            row_max(i)
+            exponent(i)
+            if i == LAST - 1:
+                invert(0)
+
         own_product(0)
         own_product(1)
         invert(1)
@@ -239,6 +237,7 @@ def tile_mix_shares_carry_slot_rows_kernel(
         invert(2)
         weigh(1)
         own_product(2)
+
         turn(1)
         invert(3)
         weigh(2)
@@ -249,19 +248,19 @@ def tile_mix_shares_carry_slot_rows_kernel(
         weigh(3)
         gather(2)
         turn(3)
-        quantize(1)
-        mix(1)
-        quantize(2)
-        mix(2)
-        own_product(3)
-        store(0, 0, False)
-        store(0, 1, False)
-        gather(3)
-        store(1, 0, True)
-        quantize(3)
-        store(1, 1, True)
-        mix(3)
-        store(2, 0, False)
-        store(2, 1, False)
-        store(3, 0, False)
-        store(3, 1, True)
+        for i in (1, 2):
+            quantize(i)
+            mix(i)
+
+        own_product(LAST)
+        store(0, 0, on_scalar, nc.sync)
+        store(0, 1, on_scalar, nc.sync)
+        gather(LAST)
+        store(1, 0, on_vector, nc.sync)
+        quantize(LAST)
+        store(1, 1, on_vector, nc.sync)
+        mix(LAST)
+        store(2, 0, on_scalar, nc.sync)
+        store(2, 1, on_scalar, nc.sync)
+        store(LAST, 0, on_scalar, nc.scalar)
+        store(LAST, 1, on_vector, nc.sync)

from contextlib import ExitStack

import concourse.mybir as mybir
from concourse.masks import make_identity

K, T, J, N = 1024, 512, 512, 512
FLOPS = 2 * K * T * J + 2 * J * N * T + 2 * K * N * T

F32 = mybir.dt.float32
BF16 = mybir.dt.bfloat16
I32 = mybir.dt.int32
U32 = mybir.dt.uint32
U8 = mybir.dt.uint8
FP8X4 = mybir.dt.float8_e4m3fn_x4
FP4X4 = mybir.dt.float4_e2m1fn_x4
ACT = mybir.ActivationFunctionType
ALU = mybir.AluOpType
AX = mybir.AxisListType

P = 128
PACK = 4
PASSES = K // (P * PACK)
TOKEN_TILES = T // P
FEATURE_TILES = N // P
LAST = TOKEN_TILES - 1
QUADRANT = 32
SCALE_ROWS = 16
BF16_ONE_PAIR = 0x3F803F80
WARM_PASSES_BEFORE_SPREAD = 10
WARM_PASSES_AFTER_SPREAD = 9


def block(i):
    return slice(i * P, (i + 1) * P)


def tile_mix_shares_carry_slot_rows_kernel(
    tc, xt_words, xt_scales, ws_words, ws_scales, fj, wo_words, wo_scales, wy_words, wy_scales, out
):
    nc = tc.nc
    with ExitStack() as ctx:
        sb = ctx.enter_context(tc.tile_pool(name="sb", bufs=1))
        ps = ctx.enter_context(tc.psum_pool(name="ps", bufs=1))
        ctx.enter_context(tc.manual_schedule())

        xt_halves = [sb.tile([P, PASSES, T // 2], U32, name="xt_half%d" % h, align_bytes=64) for h in range(2)]
        ws_codes = sb.tile([P, PASSES, 2 * J], U8, align_bytes=64)
        wy_codes = sb.tile([P, PASSES, 2 * N], U8, align_bytes=64)
        wo_codes = sb.tile([P, N], U32, align_bytes=64)
        xt_plane = sb.tile([P, PASSES, T], U8, align_bytes=64)
        ws_plane = sb.tile([P, PASSES, J], U8, align_bytes=64)
        wy_plane = sb.tile([P, PASSES, N], U8, align_bytes=64)
        wo_plane = sb.tile([P, 1, N], U8, align_bytes=64)
        fj_cols = sb.tile([P, PACK], F32)
        ident = sb.tile([P, P], F32)

        def load_scales(plane, scales, r):
            nc.sync.dma_start(
                out=plane[r:P:QUADRANT].bitcast(I32),
                in_=scales[:, r:SCALE_ROWS:PACK, :].rearrange("z q c -> q z c").bitcast(I32),
            )

        def load_tokens(h):
            words = xt_words[:, :, h * (T // 2) : (h + 1) * (T // 2), :].rearrange("z p c r -> p z (c r)")
            nc.sync.dma_start(out=xt_halves[h][:].bitcast(I32), in_=words.bitcast(I32))

        def xt_codes(z, i):
            return xt_halves[i // 2][:, z, block(i % 2)].bitcast(FP8X4)

        nc.sync.dma_start(out=fj_cols[:], in_=fj.rearrange("(p r) o -> p (r o)", r=PACK))
        nc.vector.memset(xt_plane[:].bitcast(U32), 0)
        nc.vector.memset(ws_plane[:].bitcast(U32), 0)
        for r in range(2):
            load_scales(xt_plane, xt_scales, r)
        load_tokens(0)
        nc.sync.dma_start(out=ws_codes[:].bitcast(I32), in_=ws_words.rearrange("z p c -> p z c").bitcast(I32))
        for r in range(3):
            load_scales(ws_plane, ws_scales, r)
        for r in range(2, PACK):
            load_scales(xt_plane, xt_scales, r)
        load_scales(ws_plane, ws_scales, 3)

        ones = sb.tile([P, PACK * P], BF16, align_bytes=64)
        ones_codes = sb.tile([P, P], U32, align_bytes=64)
        ones_plane = sb.tile([P, P], U8, align_bytes=64)
        nc.gpsimd.memset(ones[:].bitcast(U32), BF16_ONE_PAIR)
        nc.vector.quantize_mx(out=ones_codes[:].bitcast(FP8X4), scales=ones_plane[:], in_=ones[:])
        nc.vector.memset(ident[:], 0.0)
        make_identity(nc, ident[:], nomemset=True)
        nc.vector.memset(wy_plane[:].bitcast(U32), 0)
        nc.vector.memset(wo_plane[:].bitcast(U32), 0)

        load_tokens(1)
        nc.sync.dma_start(out=wy_codes[:].bitcast(I32), in_=wy_words.rearrange("z p c -> p z c").bitcast(I32))
        for r in range(PACK):
            load_scales(wy_plane, wy_scales, r)
        nc.sync.dma_start(out=wo_codes[:].bitcast(I32), in_=wo_words[0].rearrange("p c r -> p (c r)").bitcast(I32))
        for r in range(PACK):
            load_scales(wo_plane, wo_scales, r)

        warm_sums = ps.tile([P, P], F32, tag="bank6")

        def warm_up(passes):
            for n in range(passes):
                nc.tensor.matmul_mx(
                    out=warm_sums[:],
                    lhsT=ones_codes[:].bitcast(FP8X4),
                    lhsT_scale=ones_plane[:],
                    rhs=ones_codes[:].bitcast(FP8X4),
                    rhs_scale=ones_plane[:],
                    start=True,
                    stop=True,
                )

        warm_up(WARM_PASSES_BEFORE_SPREAD)
        fj_spread = ps.tile([P, PACK, P], F32, tag="bank7")
        for r in range(PACK):
            nc.tensor.transpose(fj_spread[:, r, :], fj_cols[:, r : r + 1].to_broadcast([P, P]), ident[:])
        fj_rows = sb.tile([P, J], F32)
        nc.scalar.copy(
            out=fj_rows[:].rearrange("t (u p e) -> t u p e", u=2, e=2),
            in_=fj_spread[:].rearrange("t (u e) p -> t u p e", u=2),
        )
        warm_up(WARM_PASSES_AFTER_SPREAD)

        scores, neg_max, expo, total, inv, qw, turned, grouped, qw_codes, qw_plane, sums = (dict() for d in range(11))

        def score(i):
            scores[i] = ps.tile([P, J], F32, name="scores%d" % i, tag="bank%d" % i)
            for z in range(PASSES):
                nc.tensor.matmul_mx(
                    out=scores[i][:],
                    lhsT=xt_codes(z, i),
                    lhsT_scale=xt_plane[:, z, block(i)],
                    rhs=ws_codes[:, z, :].bitcast(FP4X4),
                    rhs_scale=ws_plane[:, z, :],
                    start=(z == 0),
                    stop=(z == PASSES - 1),
                )

        def row_max(i):
            neg_max[i] = sb.tile([P, 1], F32, name="neg_max%d" % i)
            nc.vector.tensor_reduce(out=neg_max[i][:], in_=scores[i][:], axis=AX.X, op=ALU.max, negate=True)

        def exponent(i):
            expo[i] = sb.tile([P, J], F32, name="expo%d" % i)
            total[i] = sb.tile([P, 1], F32, name="total%d" % i)
            nc.scalar.activation(
                out=expo[i][:].rearrange("t (u p e) -> t u p e", u=2, e=2),
                in_=scores[i][:].rearrange("t (p u e) -> t u p e", u=2, e=2),
                func=ACT.Exp,
                bias=neg_max[i][:],
                accum_out=total[i][:],
            )

        def invert(i):
            inv[i] = sb.tile([P, 1], F32, name="inv%d" % i)
            nc.vector.reciprocal(out=inv[i][:], in_=total[i][:])

        def weigh(i):
            qw[i] = sb.tile([P, J], BF16, name="qw%d" % i)
            nc.vector.scalar_tensor_tensor(
                out=qw[i][:], in0=expo[i][:], scalar=inv[i][:], in1=fj_rows[:], op0=ALU.mult, op1=ALU.mult
            )

        def turn(i):
            turned[i] = ps.tile([P, 2, P], F32, name="turned%d" % i, tag="bank%d" % i)
            pairs = qw[i][:].bitcast(F32)
            for u in range(2):
                nc.tensor.transpose(turned[i][:, u, :], pairs[:, block(u)], ident[:])

        def gather(i):
            grouped[i] = sb.tile([P, PACK * P], BF16, name="grouped%d" % i, align_bytes=64)
            nc.scalar.copy(
                out=grouped[i][:].bitcast(F32).rearrange("p (t u) -> p t u", u=2),
                in_=turned[i][:].rearrange("p u t -> p t u"),
            )

        def quantize(i):
            qw_codes[i] = sb.tile([P, P], U32, name="qw_codes%d" % i, align_bytes=64)
            qw_plane[i] = sb.tile([P, P], U8, name="qw_plane%d" % i, align_bytes=64)
            nc.vector.quantize_mx(out=qw_codes[i][:].bitcast(FP8X4), scales=qw_plane[i][:], in_=grouped[i][:])

        def own_product(i):
            banks = [TOKEN_TILES + i] if i < LAST else [TOKEN_TILES + i, 0]
            per_bank = FEATURE_TILES // len(banks)
            sums[i] = [ps.tile([P, per_bank, P], F32, name="sums%d_%d" % (i, b), tag="bank%d" % b) for b in banks]
            for m in range(FEATURE_TILES):
                for z in range(PASSES):
                    nc.tensor.matmul_mx(
                        out=sums[i][m // per_bank][:, m % per_bank, :],
                        lhsT=wy_codes[:, z, 2 * P * m : 2 * P * (m + 1)].bitcast(FP4X4),
                        lhsT_scale=wy_plane[:, z, block(m)],
                        rhs=xt_codes(z, i),
                        rhs_scale=xt_plane[:, z, block(i)],
                        start=(m % per_bank == 0 and z == 0),
                        stop=False,
                    )

        def mix(i):
            per_bank = FEATURE_TILES // len(sums[i])
            for m in range(FEATURE_TILES):
                nc.tensor.matmul_mx(
                    out=sums[i][m // per_bank][:, m % per_bank, :],
                    lhsT=wo_codes[:, block(m)].bitcast(FP8X4),
                    lhsT_scale=wo_plane[:, 0, block(m)],
                    rhs=qw_codes[i][:].bitcast(FP8X4),
                    rhs_scale=qw_plane[i][:],
                    start=False,
                    stop=(m % per_bank == per_bank - 1),
                )

        out_tiles = out.rearrange("(m p) t -> p m t", p=P)

        def store(i, h, copy, queue):
            per_bank = FEATURE_TILES // len(sums[i])
            result = sb.tile([P, 2, P], F32, name="result%d_%d" % (i, h))
            bank, first = divmod(2 * h, per_bank)
            copy(out=result[:], in_=sums[i][bank][:, first : first + 2, :])
            queue.dma_start(out=out_tiles[:, 2 * h : 2 * h + 2, block(i)], in_=result[:])

        on_scalar, on_vector = nc.scalar.copy, nc.vector.tensor_copy

        for i in range(TOKEN_TILES):
            score(i)
            row_max(i)
            exponent(i)
            if i == LAST - 1:
                invert(0)

        own_product(0)
        own_product(1)
        invert(1)
        weigh(0)
        turn(0)
        gather(0)
        invert(2)
        weigh(1)
        own_product(2)

        turn(1)
        invert(3)
        weigh(2)
        turn(2)
        gather(1)
        quantize(0)
        mix(0)
        weigh(3)
        gather(2)
        turn(3)
        for i in (1, 2):
            quantize(i)
            mix(i)

        own_product(LAST)
        store(0, 0, on_scalar, nc.sync)
        store(0, 1, on_scalar, nc.sync)
        gather(LAST)
        store(1, 0, on_vector, nc.sync)
        quantize(LAST)
        store(1, 1, on_vector, nc.sync)
        mix(LAST)
        store(2, 0, on_scalar, nc.sync)
        store(2, 1, on_scalar, nc.sync)
        store(LAST, 0, on_scalar, nc.scalar)
        store(LAST, 1, on_vector, nc.sync)
